import numpy as np, ml_dtypes
CORES = [4,20,36,52,68,84,100,116,132,148,164,180,196,212,228,244]
N = 16
NP, NBK, TK, CAP = 8, 8, 64, 11
DEST = [[12,9,14,14,13,11,9,11],[9,12,11,8,13,12,15,12],[13,12,10,8,9,11,9,15],[8,8,11,10,11,9,14,8],[11,12,12,10,13,15,12,15],[11,15,14,14,14,9,11,11],[8,15,9,13,11,15,8,13],[8,12,12,8,10,8,10,12]]
def setup_inputs(rng):
    return {"x": rng.standard_normal((N, 128, NBK * TK), dtype=np.float32).astype(ml_dtypes.bfloat16), "w": (rng.standard_normal((N, 128, 128), dtype=np.float32) / 8).astype(ml_dtypes.bfloat16)}
def setup_inputs_big(rng):
    d = setup_inputs(rng)
    for k in ("x", "w"): d[k] = (d[k].astype(np.float32) * 1024.0).astype(d[k].dtype)
    return d
def setup_inputs_small(rng):
    d = setup_inputs(rng)
    for k in ("x", "w"): d[k] = (d[k].astype(np.float32) * (1 / 1024.0)).astype(d[k].dtype)
    return d
def reference(x, w):
    X, W = x.astype(np.float64), w.astype(np.float64)
    y = np.full((N, 128, CAP * TK), np.nan); n = [0] * N
    for p in range(NP):
        for c in range(NBK):
            q = DEST[p][c]
            y[q][:, TK * n[q]:TK * n[q] + TK] = W[q].T @ np.maximum(W[p].T @ X[p][:, TK * c:TK * c + TK], 0.0)
            n[q] += 1
    return {"y": y.astype(ml_dtypes.bfloat16 if x.dtype != np.float64 else np.float64)}

from concourse.bass import DstId, RemoteDMATransfer
from concourse.mybir import AluOpType

TK = 64
NBK = 8
CAP = 11
BANKS = 8

SCRATCH = {
    "ws": ("sbuf", [128, 128], "bfloat16"),
    "xs": ("sbuf", [128, NBK * TK], "bfloat16"),
    "zero": ("sbuf", [128, 512], "float32"),
    "hs": ("sbuf", [128, NBK * TK], "bfloat16"),
    "land": ("sbuf", [128, CAP * TK], "bfloat16"),
    "ys": ("sbuf", [128, CAP * TK], "bfloat16"),
}
for _b in range(BANKS):
    SCRATCH["ps%d" % _b] = ("psum", [128, 512], "float32")

SEMAPHORES = (["ld0", "ld1", "zs", "sent", "st"] + ["mm%d" % i for i in range(BANKS)] + ["rl%d" % i for i in range(BANKS)]
              + ["cp%d" % i for i in range(BANKS)] + ["arr%d" % i for i in range(8)])


def _groups(dest):
    fill, out = {}, []
    for row in dest:
        blocks, order = {}, []
        for c, q in enumerate(row):
            if q not in blocks:
                blocks[q] = []
                order.append(q)
            blocks[q].append(c)
        lst = []
        for q in order:
            lst.append((q, tuple(blocks[q]), fill.get(q, 0)))
            fill[q] = fill.get(q, 0) + len(blocks[q])
        out.append(lst)
    return out, fill


def _subsets(items, k):
    if k == 0:
        return [[]]
    res = []
    for i in range(len(items) - k + 1):
        for tail in _subsets(items[i + 1:], k - 1):
            res.append([items[i]] + tail)
    return res


def _calls(writes, load, lanes):
    byw = {}
    for wr in writes:
        byw.setdefault(len(wr[1]), []).append(wr)
    best = None
    for w in sorted(byw):
        n = len(byw[w])
        k = min(n & -n, lanes)
        for sub in _subsets(byw[w], k):
            cs = [c for wr in sub for c in wr[1]]
            key = (max(cs) - min(cs) + 1, k * w, min(cs))
            if best is None or key < best[0]:
                best = (key, sub)
    first = best[1]
    rest = []
    for w in sorted(byw):
        left = sorted([wr for wr in byw[w] if wr not in first], key=lambda wr: (-load[wr[0]], wr[0]))
        k = lanes
        while left:
            while k > len(left):
                k //= 2
            rest.append(left[:k])
            left = left[k:]
    rest.sort(key=lambda call: (-max(load[wr[0]] for wr in call), -len(call[0][1]), call[0][0]))
    return [first] + rest


def _engines(topo, src, dsts):
    m = topo.mask(src, dsts[0])
    for d in dsts:
        m &= topo.mask(src, d)
    return [e for e in range(16) if (m >> e) & 1]


def _plan(T, topo):
    dest = T.tables["DEST"]
    writes, load = _groups(dest)
    calls, due = [], {}
    for p, lst in enumerate(writes):
        eng = _engines(topo, T.cores[p], [T.cores[wr[0]] for wr in lst])
        cl = _calls(lst, load, len(eng))
        calls.append((cl, eng))
        t = 0
        for call in cl:
            t += 128 * len(call) // len(eng) * (4 + len(call[0][1]))
            for q, cs, slot in call:
                due[(p, q)] = (t, p, slot, len(cs), len(eng) // len(call))
    return calls, due


def _sender(g, core, T, topo, calls, eng):
    sem = T.sem
    assert len(calls) <= BANKS
    cs0 = [c for wr in calls[0] for c in wr[1]]
    lo, hi = min(cs0) * TK, (max(cs0) + 1) * TK
    g.sync.dma_start(T.ws[:], T.w[:]).then_inc(sem.ld0, 16)
    g.scalar.dma_start(T.xs[:, lo:hi], T.x[:, lo:hi]).then_inc(sem.ld0, 16)
    n1 = 0
    if hi < NBK * TK:
        g.scalar.dma_start(T.xs[:, hi:], T.x[:, hi:]).then_inc(sem.ld1, 16)
        n1 += 16
    if lo > 0:
        g.sync.dma_start(T.xs[:, :lo], T.x[:, :lo]).then_inc(sem.ld1, 16)
        n1 += 16
    widest = max(len(call) * len(call[0][1]) for call in calls) * TK
    g.vector.memset(T.zero[:, :widest], 0.0).then_inc(sem.zs, 1)
    g.vector.wait_ge(sem.zs, 1)
    g.tensor.wait_ge(sem.ld0, 32)
    base = 0
    for j, call in enumerate(calls):
        ps = T["ps%d" % j]
        if j == 1 and n1:
            g.tensor.wait_ge(sem.ld1, n1)
        cs = [c for wr in call for c in wr[1]]
        for k, c in enumerate(cs):
            g.tensor.matmul(ps[:, k * TK:(k + 1) * TK], T.ws[:], T.xs[:, c * TK:(c + 1) * TK], True, True).then_inc(
                sem["mm%d" % j], 1)
        n = len(cs) * TK
        g.vector.wait_ge(sem["mm%d" % j], len(cs))
        g.vector.tensor_tensor(T.hs[:, base:base + n], ps[:, :n], T.zero[:, :n], AluOpType.max).then_inc(sem["rl%d" % j], 1)
        g.wait_ge(sem["rl%d" % j], 1)
        share = len(eng) // len(call)
        trs = []
        for i, (q, blocks, slot) in enumerate(call):
            d = T.cores[q]
            assert topo.may_write(core, d)
            rid, pid = topo.addr(d, core)
            w = len(blocks) * TK
            m = 0
            for e in eng[i * share:(i + 1) * share]:
                m |= 1 << e
            trs.append(RemoteDMATransfer(dst_ids=[DstId(rid=rid, pnc=pid)], dma_engine_mask=m,
                                         remote_sem=sem["arr%d" % T.rank_of(core)],
                                         src=T.hs[:, base + i * w:base + (i + 1) * w],
                                         dst=T.land[:, slot * TK:slot * TK + w]))
        g.remote_dma_fused(trs, local_sem=sem.sent)
        base += n
    g.wait_ge(sem.sent, len(calls) * len(eng))


def _owner(g, T, mine):
    sem = T.sem
    assert len(mine) <= BANKS
    g.sync.dma_start(T.ws[:], T.w[:]).then_inc(sem.ld0, 16)
    g.tensor.wait_ge(sem.ld0, 16)
    for j, (_, p, slot, k, ne) in enumerate(mine):
        ps = T["ps%d" % j]
        a, b = slot * TK, (slot + k) * TK
        g.tensor.wait_ge(sem["arr%d" % p], ne)
        g.tensor.matmul(ps[:, :b - a], T.ws[:], T.land[:, a:b], True, True).then_inc(sem["mm%d" % j], 1)
        g.vector.wait_ge(sem["mm%d" % j], 1)
        g.vector.tensor_copy(T.ys[:, a:b], ps[:, :b - a]).then_inc(sem["cp%d" % j], 1)
    last = len(mine) - 1
    early = []
    for side in (lambda s: s < mine[last][2], lambda s: s > mine[last][2]):
        js = [j for j in range(last) if side(mine[j][2])]
        if js:
            early.append(js)
    early.sort(key=max)
    queues = [g.scalar, g.sync]
    parts = [(js, queues[i % 2]) for i, js in enumerate(early)] + [([last], g.scalar)]
    for js, qu in parts:
        for j in js:
            qu.wait_ge(sem["cp%d" % j], 1)
        a = min(mine[j][2] for j in js) * TK
        b = max(mine[j][2] + mine[j][3] for j in js) * TK
        qu.dma_start(T.y[:, a:b], T.ys[:, a:b]).then_inc(sem.st, 16)
    g.wait_ge(sem.st, 16 * len(parts))


def rank_program(g, core, T, topo):
    rank = T.rank_of(core)
    if rank is None:
        return
    calls, due = _plan(T, topo)
    if rank < len(calls):
        _sender(g, core, T, topo, calls[rank][0], calls[rank][1])
    else:
        _owner(g, T, sorted(v for (p, q), v in due.items() if q == rank))
